import numpy as np
import ml_dtypes


def mxq(x, axis, fmt="e4m3"):
    dtype, down = {"e4m3": (ml_dtypes.float8_e4m3fn, 7), "e5m2": (ml_dtypes.float8_e5m2, 14)}[fmt]
    v = np.moveaxis(np.asarray(x, np.float32).astype(ml_dtypes.bfloat16).astype(np.float64), axis, -1)
    blocks = v.reshape(v.shape[:-1] + (-1, 32))
    amax = np.abs(blocks).max(-1, keepdims=True)
    byte = np.maximum(np.where(amax > 0, np.frexp(amax)[1] - 1 + 127, 0) - down, 1)
    scale = np.exp2(byte - 127.0)
    codes = (blocks / scale).astype(np.float32).astype(dtype).astype(np.float64)
    return np.moveaxis((codes * scale).reshape(v.shape), -1, axis)


WIDE = False


def mx_kscale(k):
    if not WIDE:
        return np.ones(k)
    levels = np.array([10, -10, 5, -5, 0])
    if k % 512:
        return np.exp2(np.random.permutation(np.resize(levels, k // 32))).repeat(32)
    a = np.empty((k // 512, 16))
    for p in range(k // 512):
        a[p, :8] = np.random.permutation(np.resize(levels, 8))
        for g in range(8):
            far = levels[np.abs(levels - a[p, g]) >= 10]
            a[p, g + 8] = far[np.random.randint(len(far))]
    return np.exp2(a.ravel()).repeat(32)


def f64(x):
    return np.asarray(x).astype(np.float64)


def striped(idx):
    return np.tile(idx.reshape(-1, 16).T, (8, 1)).astype(np.uint16)


def unstriped(offs):
    return offs[:16].T.reshape(-1).astype(np.int64)


def striped8(idx):
    return np.concatenate([x.reshape(-1, 16).T for x in idx]).astype(np.uint16)


def runs(offs, k):
    lists = np.stack([offs[16 * r : 16 * r + 16].T.reshape(-1) for r in range(8)]).astype(np.int64)
    return lists[np.arange(k) % 512 // 64]


def pack_weight(w):
    k, n = w.shape
    w = f64(np.asarray(w, np.float32).astype(ml_dtypes.bfloat16)).reshape(k // 32, 32, n)
    amax = np.abs(w).max(1)
    byte = np.clip(np.where(amax > 0, np.frexp(amax)[1] - 1 + 127 - 7, 1), 1, 254)
    scaled = (w * np.exp2(127.0 - byte)[:, None, :]).reshape(k, n).astype(np.float32)
    words = np.ascontiguousarray(scaled.reshape(k // 512, 128, 4, n).transpose(0, 1, 3, 2)).astype(ml_dtypes.float8_e4m3fn).view(np.uint8)
    return words, np.ascontiguousarray(byte.astype(np.uint8).reshape(k // 512, 16, n))


def unpack_weight(words, scales):
    g, p, n, _ = words.shape
    vals = np.ascontiguousarray(words).view(ml_dtypes.float8_e4m3fn).astype(np.float64) * np.repeat(np.exp2(scales.astype(np.float64) - 127.0), 8, axis=1)[..., None]
    return vals.transpose(0, 1, 3, 2).reshape(g * 512, n)

def planes(y):
    n, m = y.shape
    v = y.astype(np.float32).astype(ml_dtypes.bfloat16).astype(np.float64).reshape(n // 32, 32, m)
    top = np.abs(v).max(1)
    byte = np.clip(np.where(top > 0, np.frexp(top)[1] - 1 + 127 - 7, 1), 1, 254)
    codes = (v * np.exp2(127.0 - byte)[:, None, :]).reshape(n, m).astype(np.float32).astype(ml_dtypes.float8_e4m3fn).view(np.uint8)
    words = codes.reshape(n // 512, 128, 4, m).transpose(0, 1, 3, 2)
    return np.ascontiguousarray(words), np.ascontiguousarray(byte.astype(np.uint8).reshape(n // 512, 16, m))


K, T, S, N, H, W = 512, 2048, 256, 512, 512, 192


def setup_inputs():
    n = np.random.standard_normal
    s = mx_kscale(K)[:, None]
    u = mx_kscale(H)
    packed_xT = pack_weight(n((K, T)) * s)
    packed_w1 = pack_weight(n((K, H)) / np.sqrt(K) / s)
    packed_w2 = pack_weight(n((K, H)) / np.sqrt(K) / s)
    packed_w3 = pack_weight(n((H, N)) / np.sqrt(2 * H) / u[:, None])
    packed_w4 = pack_weight(n((H, N)) / np.sqrt(2 * H) / u[:, None])
    return {
        "x_words": packed_xT[0],
        "x_scales": packed_xT[1],
        "w1_words": packed_w1[0],
        "w1_scales": packed_w1[1],
        "w2_words": packed_w2[0],
        "w2_scales": packed_w2[1],
        "gn": (np.random.uniform(0.5, 1.5, (H, 1)) * u[:, None]).astype(np.float32),
        "gm": (np.random.uniform(0.5, 1.5, (H, 1)) * u[:, None]).astype(np.float32),
        "w3_words": packed_w3[0],
        "w3_scales": packed_w3[1],
        "w4_words": packed_w4[0],
        "w4_scales": packed_w4[1],
        "offs": striped(np.random.permutation(T)[:S]),
        "hz": striped8(np.random.randint(0, T, (8, S))),
        "n1": striped(np.random.permutation(S)[:W]),
        "n2": striped(np.random.permutation(S)[:W]),
        "n3": striped(np.random.permutation(S)),
        "n4": striped(np.random.permutation(S)),
        "n5": striped(np.random.permutation(S)),
    }


def reference(x_words, x_scales, w1_words, w1_scales, w2_words, w2_scales, gn, gm, w3_words, w3_scales, w4_words, w4_scales, offs, hz, n1, n2, n3, n4, n5):
    xq = unpack_weight(x_words, x_scales)[:, unstriped(offs)]
    y = unpack_weight(w1_words, w1_scales).T @ xq
    pa = y[:, unstriped(n2)]
    old = y[:, unstriped(n1)]
    ra = np.maximum(pa, 0.5 * old)
    ds = y.copy()
    ds[:, unstriped(n1)] = ra
    z = f64(gn) * ds
    x_hz = unpack_weight(x_words, x_scales)[np.arange(K)[:, None], runs(hz, K)]
    d = unpack_weight(w2_words, w2_scales).T @ x_hz
    st = np.maximum(d, d[:, unstriped(n3)])
    z2 = f64(gm) * (np.minimum(st, st[:, unstriped(n4)]))
    h = unpack_weight(w3_words, w3_scales).T @ mxq(z, 0, "e4m3") + unpack_weight(w4_words, w4_scales).T @ mxq(z2, 0, "e4m3")
    out_0 = h - h[:, unstriped(n5)]
    return (out_0,) + planes(out_0)

@@ -1,0 +1,255 @@
+from contextlib import ExitStack
+
+import concourse.mybir as mybir
+
+K, T, S, H, N, W = 512, 2048, 256, 512, 512, 192
+FLOPS = 4 * 2 * K * H * S
+
+F32 = mybir.dt.float32
+BF16 = mybir.dt.bfloat16
+I32 = mybir.dt.int32
+U32 = mybir.dt.uint32
+U16 = mybir.dt.uint16
+U8 = mybir.dt.uint8
+FP8X4 = mybir.dt.float8_e4m3fn_x4
+ALU = mybir.AluOpType
+COPY = mybir.ActivationFunctionType.Copy
+
+P = 128
+PACK = 4
+HALF = S // 2
+SPARE = 16
+
+
+def tile_picked_hjoinkmaxhopmndif_none_po_kernel(
+    tc, x_words, x_scales, w1_words, w1_scales, w2_words, w2_scales, gn, gm,
+    w3_words, w3_scales, w4_words, w4_scales, offs, hz, n1, n2, n3, n4, n5,
+    out_0, out_1, out_2,
+):
+    nc = tc.nc
+    with ExitStack() as ctx:
+        keep = ctx.enter_context(tc.tile_pool(name="keep", bufs=1))
+        shared = ctx.enter_context(tc.tile_pool(name="shared", bufs=1))
+        psum = ctx.enter_context(tc.psum_pool(name="psum", bufs=1))
+
+        def sb(name, shape, dtype):
+            return keep.tile(shape, dtype, name=name, align_bytes=64)
+
+        def load_list(name, src):
+            tile = keep.tile(list(src.shape), U16, name=name)
+            nc.sync.dma_start(tile[:], src)
+            return tile
+
+        def load_words(queue, name, src, tag=None):
+            tile = keep.tile([P, src.shape[2]], U32, name=name, tag=tag or name, align_bytes=64)
+            queue.dma_start(tile[:].bitcast(I32), src[0].rearrange("p c r -> p (c r)").bitcast(I32))
+            return tile
+
+        def deal(name, src, dtype, run, tag=None):
+            tile = keep.tile([P, H], dtype, name=name, tag=tag or name, align_bytes=64)
+            nc.vector.tensor_copy(
+                out=tile[:].rearrange("p (t c i) -> p c t i", t=PACK, i=run),
+                in_=src[:].rearrange("p (c i t) -> p c t i", t=PACK, i=run),
+            )
+            return tile
+
+        def s_copy(out, in_):
+            nc.scalar.activation(out, in_, COPY)
+
+        def product(acc, words, scales, row0, t, rhs, rhs_scale, start, stop):
+            cols = slice(P * t, P * (t + 1))
+            nc.tensor.matmul_mx(
+                out=acc, lhsT=words[:, cols].bitcast(FP8X4), lhsT_scale=scales[row0:P, cols],
+                rhs=rhs[:].bitcast(FP8X4), rhs_scale=rhs_scale[:], start=start, stop=stop,
+            )
+
+        def reused(name, tag, shape, dtype):
+            return keep.tile(shape, dtype, name=name, tag=tag, align_bytes=64)
+
+        def stage_scales(queue, stage, w, src):
+            queue.dma_start(stage[w:32:8, :], src[0].rearrange("(q r) c -> q (r c)", r=4).bitcast(I32))
+
+        def spread_scales(queue, tile, stage):
+            queue.dma_start(tile[:].bitcast(I32), stage[:].rearrange("g (r c) -> g r c", r=4))
+
+        def flat(tile):
+            return tile[:].rearrange("p a j -> p (a j)")
+
+        xs = sb("xs", [P, T], U8)
+        nc.vector.memset(xs[:].bitcast(I32), 0)
+        stage1 = sb("stage1", [32, H], I32)
+        nc.vector.memset(stage1[:], 0)
+        d_sb = [reused("d_sb%d" % t, "d%d" % t, [P, S + SPARE], F32) for t in range(PACK)]
+        st_sb = [sb("st_sb%d" % u, [P, 3 * S], F32) for u in range(2)]
+        for tile in d_sb:
+            nc.vector.memset(tile[:, S:], 0.0)
+        for tile in st_sb:
+            nc.vector.memset(tile[:, 2 * S :], 0.0)
+
+        l_offs = load_list("l_offs", offs)
+        l_hz = load_list("l_hz", hz)
+        xs_rows = x_scales[0].bitcast(I32)
+        xs_i = xs[:].bitcast(I32)
+        w1w = load_words(nc.gpsimd, "w1w", w1_words)
+        for r in range(2):
+            nc.scalar.dma_start(xs_i[r:P:32, :], xs_rows[r:16:4, :])
+        for r, queue in ((2, nc.scalar), (3, nc.sync)):
+            queue.dma_start(xs_i[r:P:16, :], xs_rows[r:16:4, :].unsqueeze(1).broadcast_to([4, 2, T // 4]))
+        stage_scales(nc.sync, stage1, 0, w1_scales)
+        xw = load_words(nc.sync, "xw", x_words)
+        l_n2 = load_list("l_n2", n2)
+        l_n1 = load_list("l_n1", n1)
+        l_n3 = load_list("l_n3", n3)
+        g_n = sb("g_n", [P, PACK], F32)
+        g_m = sb("g_m", [P, PACK], F32)
+        nc.gpsimd.dma_start(g_m[:], gm.rearrange("(p t) o -> p (t o)", t=PACK))
+        nc.gpsimd.dma_start(g_n[:], gn.rearrange("(p t) o -> p (t o)", t=PACK))
+        stage234 = reused("stage234", "stage234", [32, H], I32)
+        nc.gpsimd.memset(stage234[:], 0)
+        w2w = load_words(nc.gpsimd, "w2w", w2_words)
+        s1 = reused("s1", "s1", [P, H], U8)
+        spread_scales(nc.scalar, s1, stage1)
+        for w, src in enumerate((w2_scales, w3_scales, w4_scales)):
+            stage_scales(nc.scalar, stage234, w, src)
+
+        xs_offs = sb("xs_offs", [P, S], U8)
+        nc.vector.tensor_copy(xs_offs[:], xs[:].indirect(l_offs[:]))
+        xs_hz = sb("xs_hz", [P, S], U8)
+        nc.vector.tensor_copy(xs_hz[:], xs[:].indirect(l_hz[:]))
+        xs_hz_placed = sb("xs_hz_placed", [P, S], U8)
+        nc.vector.tensor_copy(xs_hz_placed[:].bitcast(I32), xs_hz[:].bitcast(I32))
+        for r in range(2, 4):
+            nc.scalar.dma_start(xs_hz_placed[:].bitcast(I32)[r:P:32, :], xs_hz[:].bitcast(I32)[16 + r : P : 32, :])
+        s234 = shared.tile([P, H], U8, name="s234", offset=4 * S - H // 2, align_bytes=64)
+        spread_scales(nc.sync, s234, stage234)
+        l_n4 = load_list("l_n4", n4)
+        l_n5 = load_list("l_n5", n5)
+
+        xw_offs = sb("xw_offs", [P, S], U32)
+        nc.vector.tensor_copy(xw_offs[:], xw[:].indirect(l_offs[:]))
+        s1d = deal("s1d", s1, U8, 16)
+        w1d = deal("w1d", w1w, U32, 4)
+        xw_hz = reused("xw_hz", "s1", [P, S], U32)
+        nc.vector.tensor_copy(xw_hz[:], xw[:].indirect(l_hz[:]))
+        w2d = deal("w2d", w2w, U32, 4, "xw")
+        w4w = load_words(nc.sync, "w4w", w4_words, "w2w")
+        w3w = load_words(nc.sync, "w3w", w3_words, "stage234")
+        s234d = deal("s234d", s234, U8, 16)
+
+        y_ps = [psum.tile([P, S], F32, name="y_ps%d" % t, tag="bank%d" % t) for t in range(PACK)]
+        d_ps = [psum.tile([P, S], F32, name="d_ps%d" % t) for t in range(PACK)]
+        y_sb = [sb("y_sb%d" % t, [P, S], F32) for t in range(2)]
+        y_sb += [shared.tile([P, S], F32, name="y_sb%d" % t, offset=4 * S * (t - 2), align_bytes=64) for t in (2, 3)]
+        for t in range(PACK):
+            product(y_ps[t][:], w1d, s1d, 0, t, xw_offs, xs_offs, True, True)
+        for t in range(PACK):
+            product(d_ps[t][:], w2d, s234d, 0, t, xw_hz, xs_hz_placed, True, True)
+        nc.scalar.copy(y_sb[0][:], y_ps[0][:])
+        nc.vector.tensor_copy(y_sb[1][:], y_ps[1][:])
+        for t in range(PACK):
+            nc.vector.tensor_copy(d_sb[t][:, :S], d_ps[t][:])
+        for t in range(2, PACK):
+            nc.vector.tensor_copy(y_sb[t][:], y_ps[t][:])
+
+        d_n3 = [sb("d_n3%d" % u, [P, 2, S], F32) for u in range(2)]
+        st_n4 = [reused("st_n4%d" % u, "n4%d" % u, [P, 2, S], F32) for u in range(2)]
+        low = sb("low", [P, PACK, S], F32)
+        picked = [sb("picked0", [P, 2, 2, W], F32)]
+
+        def pick(t):
+            s_copy(picked[t // 2][:, 0, t % 2, :], y_sb[t][:].indirect(l_n2[:]))
+            s_copy(picked[t // 2][:, 1, t % 2, :], y_sb[t][:].indirect(l_n1[:]))
+
+        pick(0)
+        for t in range(PACK):
+            s_copy(d_n3[t // 2][:, t % 2, :], d_sb[t][:].indirect(l_n3[:]))
+        pick(1)
+        picked.append(reused("picked1", "d3", [P, 2, 2, W], F32))
+        pick(2)
+        pick(3)
+        w3d = deal("w3d", w3w, U32, 4)
+        w4d = deal("w4d", w4w, U32, 4)
+        ra = [reused("ra0", "d1", [P, 2, W], F32)]
+
+        def larger(u):
+            nc.vector.scalar_tensor_tensor(
+                out=flat(ra[u]), in0=flat(picked[u][:, 1]), scalar=0.5, in1=flat(picked[u][:, 0]),
+                op0=ALU.mult, op1=ALU.max)
+
+        def upper(u):
+            for a in range(2):
+                nc.vector.tensor_tensor(st_sb[u][:, a * S : (a + 1) * S], d_ps[2 * u + a][:], d_n3[u][:, a, :], ALU.max)
+
+        def fetch(t):
+            a = t % 2
+            nc.vector.tensor_copy(st_n4[t // 2][:, a, :], st_sb[t // 2][:, a * S : (a + 2) * S].indirect(l_n4[:]))
+
+        def lower(u):
+            nc.vector.tensor_tensor(flat(low[:, 2 * u : 2 * u + 2, :]), st_sb[u][:, : 2 * S], flat(st_n4[u]), ALU.min)
+
+        upper(0)
+        larger(0)
+        fetch(0)
+        fetch(1)
+        upper(1)
+        lower(0)
+        fetch(2)
+        ra.append(reused("ra1", "n40", [P, 2, W], F32))
+        larger(1)
+        fetch(3)
+        for t in range(PACK):
+            s_copy(y_sb[t][:].indirect(l_n1[:]), ra[t // 2][:, t % 2, :])
+        lower(1)
+
+        z2_b = sb("z2_b", [P, S * PACK], BF16)
+        nc.vector.tensor_tensor(
+            z2_b[:].rearrange("p (c i t) -> p c t i", t=PACK, i=4),
+            low[:].rearrange("p t (c i) -> p c t i", i=4),
+            g_m[:].unsqueeze(1).unsqueeze(3).broadcast_to([P, S // 4, PACK, 4]),
+            ALU.mult)
+        z_b = reused("z_b", "n41", [P, S, PACK], BF16)
+        z2w = sb("z2w", [P, S], U32)
+        z2s = sb("z2s", [P, S], U8)
+        zw = sb("zw", [P, S], U32)
+        zs = sb("zs", [P, S], U8)
+        for t in range(PACK - 1):
+            nc.vector.tensor_scalar(z_b[:, :, t], y_sb[t][:], g_n[:, t : t + 1], None, ALU.mult)
+            if t == 0:
+                nc.vector.quantize_mx(out=z2w[:].bitcast(FP8X4), scales=z2s[:], in_=z2_b[:])
+        h_ps = [psum.tile([P, S], F32, name="h_ps%d" % t, tag="bank%d" % t) for t in range(PACK)]
+        for t in range(PACK):
+            product(h_ps[t][:], w4d, s234d, 8, t, z2w, z2s, True, False)
+        t = PACK - 1
+        nc.vector.tensor_scalar(z_b[:, :, t], y_sb[t][:], g_n[:, t : t + 1], None, ALU.mult)
+        nc.vector.quantize_mx(out=zw[:].bitcast(FP8X4), scales=zs[:], in_=z_b[:].rearrange("p j t -> p (j t)"))
+        for t in range(PACK):
+            product(h_ps[t][:], w3d, s234d, 4, t, zw, zs, False, True)
+
+        h_sb = sb("h_sb", [P, PACK, S], F32)
+        for t in range(PACK):
+            nc.vector.tensor_copy(h_sb[:, t, :], h_ps[t][:])
+        res = sb("res", [P, PACK, S], F32)
+        res_b = sb("res_b", [P, S * PACK], BF16)
+        res_w = sb("res_w", [P, S], U32)
+        res_s = sb("res_s", [P, S], U8)
+        out_rows = out_0.rearrange("(p t) j -> p t j", t=PACK)
+        out_words = out_1[0].rearrange("p c r -> p (c r)").bitcast(I32)
+        for half in range(2):
+            cols = slice(half * HALF, (half + 1) * HALF)
+            h_n5 = sb("h_n5%d" % half, [P, PACK, HALF], F32)
+            for t in range(PACK):
+                window = flat(h_sb)[:, t * S : (PACK if half else t + 1) * S]
+                s_copy(h_n5[:, t, :], window.indirect(l_n5[:, half * 8 : (half + 1) * 8]))
+            for pair in (slice(0, 3), slice(3, 4)) if half else (slice(0, PACK),):
+                nc.vector.tensor_tensor(res[:, pair, cols], h_sb[:, pair, cols], h_n5[:, pair, :], ALU.subtract)
+            nc.scalar.dma_start(out_rows[:, :, cols], res[:, :, cols])
+            wide = slice(half * HALF * PACK, (half + 1) * HALF * PACK)
+            nc.vector.tensor_copy(
+                res_b[:, wide].rearrange("p (c i t) -> p c t i", t=PACK, i=4),
+                res[:, :, cols].rearrange("p t (c i) -> p c t i", i=4))
+            nc.vector.quantize_mx(out=res_w[:, cols].bitcast(FP8X4), scales=res_s[:, cols], in_=res_b[:, wide])
+            nc.sync.dma_start(out_words[:, cols], res_w[:, cols].bitcast(I32))
+        out_scales = out_2[0].bitcast(I32)
+        for r in range(4):
+            queue = nc.scalar if r < 2 else nc.sync
+            queue.dma_start(out_scales[r:16:4, :], res_s[:].bitcast(I32)[r:P:32, :])

@@ -19,6 +19,7 @@ P = 128
 PACK = 4
 HALF = S // 2
 SPARE = 16
+WIDE_SPARE = 96
 
 
 def tile_picked_hjoinkmaxhopmndif_none_po_kernel(
@@ -79,38 +80,39 @@ def tile_picked_hjoinkmaxhopmndif_none_po_kernel(
         nc.vector.memset(xs[:].bitcast(I32), 0)
         stage1 = sb("stage1", [32, H], I32)
         nc.vector.memset(stage1[:], 0)
+        stage234 = reused("stage234", "stage234", [32, H], I32)
+        nc.vector.memset(stage234[:], 0)
         d_sb = [reused("d_sb%d" % t, "d%d" % t, [P, S + SPARE], F32) for t in range(PACK)]
-        st_sb = [sb("st_sb%d" % u, [P, 3 * S], F32) for u in range(2)]
+        st_sb = [sb("st_sb%d" % u, [P, S + WIDE_SPARE], F32) for u in range(2)]
         for tile in d_sb:
             nc.vector.memset(tile[:, S:], 0.0)
         for tile in st_sb:
-            nc.vector.memset(tile[:, 2 * S :], 0.0)
+            nc.vector.memset(tile[:, S:], 0.0)
 
         l_offs = load_list("l_offs", offs)
         l_hz = load_list("l_hz", hz)
         xs_rows = x_scales[0].bitcast(I32)
         xs_i = xs[:].bitcast(I32)
-        w1w = load_words(nc.gpsimd, "w1w", w1_words)
         for r in range(2):
             nc.scalar.dma_start(xs_i[r:P:32, :], xs_rows[r:16:4, :])
         for r, queue in ((2, nc.scalar), (3, nc.sync)):
             queue.dma_start(xs_i[r:P:16, :], xs_rows[r:16:4, :].unsqueeze(1).broadcast_to([4, 2, T // 4]))
         stage_scales(nc.sync, stage1, 0, w1_scales)
         xw = load_words(nc.sync, "xw", x_words)
+        for w, src in enumerate((w2_scales, w3_scales, w4_scales)):
+            stage_scales(nc.sync, stage234, w, src)
+        w1w = load_words(nc.sync, "w1w", w1_words)
         l_n2 = load_list("l_n2", n2)
+        w2w = load_words(nc.sync, "w2w", w2_words)
         l_n1 = load_list("l_n1", n1)
-        l_n3 = load_list("l_n3", n3)
+        s1 = reused("s1", "s1", [P, H], U8)
+        spread_scales(nc.scalar, s1, stage1)
+        s234 = shared.tile([P, H], U8, name="s234", offset=4 * S - H // 2, align_bytes=64)
+        spread_scales(nc.sync, s234, stage234)
         g_n = sb("g_n", [P, PACK], F32)
         g_m = sb("g_m", [P, PACK], F32)
         nc.gpsimd.dma_start(g_m[:], gm.rearrange("(p t) o -> p (t o)", t=PACK))
         nc.gpsimd.dma_start(g_n[:], gn.rearrange("(p t) o -> p (t o)", t=PACK))
-        stage234 = reused("stage234", "stage234", [32, H], I32)
-        nc.gpsimd.memset(stage234[:], 0)
-        w2w = load_words(nc.gpsimd, "w2w", w2_words)
-        s1 = reused("s1", "s1", [P, H], U8)
-        spread_scales(nc.scalar, s1, stage1)
-        for w, src in enumerate((w2_scales, w3_scales, w4_scales)):
-            stage_scales(nc.scalar, stage234, w, src)
 
         xs_offs = sb("xs_offs", [P, S], U8)
         nc.vector.tensor_copy(xs_offs[:], xs[:].indirect(l_offs[:]))
@@ -119,9 +121,10 @@ def tile_picked_hjoinkmaxhopmndif_none_po_kernel(
         xs_hz_placed = sb("xs_hz_placed", [P, S], U8)
         nc.vector.tensor_copy(xs_hz_placed[:].bitcast(I32), xs_hz[:].bitcast(I32))
         for r in range(2, 4):
-            nc.scalar.dma_start(xs_hz_placed[:].bitcast(I32)[r:P:32, :], xs_hz[:].bitcast(I32)[16 + r : P : 32, :])
-        s234 = shared.tile([P, H], U8, name="s234", offset=4 * S - H // 2, align_bytes=64)
-        spread_scales(nc.sync, s234, stage234)
+            nc.sync.dma_start(xs_hz_placed[:].bitcast(I32)[r:P:32, :], xs_hz[:].bitcast(I32)[16 + r : P : 32, :])
+        l_n3 = load_list("l_n3", n3)
+        w4w = load_words(nc.sync, "w4w", w4_words)
+        w3w = load_words(nc.sync, "w3w", w3_words)
         l_n4 = load_list("l_n4", n4)
         l_n5 = load_list("l_n5", n5)
 
@@ -129,16 +132,14 @@ def tile_picked_hjoinkmaxhopmndif_none_po_kernel(
         nc.vector.tensor_copy(xw_offs[:], xw[:].indirect(l_offs[:]))
         s1d = deal("s1d", s1, U8, 16)
         w1d = deal("w1d", w1w, U32, 4)
-        xw_hz = reused("xw_hz", "s1", [P, S], U32)
+        xw_hz = reused("xw_hz", "w1w", [P, S], U32)
         nc.vector.tensor_copy(xw_hz[:], xw[:].indirect(l_hz[:]))
         w2d = deal("w2d", w2w, U32, 4, "xw")
-        w4w = load_words(nc.sync, "w4w", w4_words, "w2w")
-        w3w = load_words(nc.sync, "w3w", w3_words, "stage234")
         s234d = deal("s234d", s234, U8, 16)
 
         y_ps = [psum.tile([P, S], F32, name="y_ps%d" % t, tag="bank%d" % t) for t in range(PACK)]
         d_ps = [psum.tile([P, S], F32, name="d_ps%d" % t) for t in range(PACK)]
-        y_sb = [sb("y_sb%d" % t, [P, S], F32) for t in range(2)]
+        y_sb = [sb("y_sb0", [P, S], F32), reused("y_sb1", "stage234", [P, S], F32)]
         y_sb += [shared.tile([P, S], F32, name="y_sb%d" % t, offset=4 * S * (t - 2), align_bytes=64) for t in (2, 3)]
         for t in range(PACK):
             product(y_ps[t][:], w1d, s1d, 0, t, xw_offs, xs_offs, True, True)
@@ -151,77 +152,91 @@ def tile_picked_hjoinkmaxhopmndif_none_po_kernel(
         for t in range(2, PACK):
             nc.vector.tensor_copy(y_sb[t][:], y_ps[t][:])
 
-        d_n3 = [sb("d_n3%d" % u, [P, 2, S], F32) for u in range(2)]
-        st_n4 = [reused("st_n4%d" % u, "n4%d" % u, [P, 2, S], F32) for u in range(2)]
-        low = sb("low", [P, PACK, S], F32)
-        picked = [sb("picked0", [P, 2, 2, W], F32)]
+        d_n3 = [reused("d_n3%d" % t, "d_n3%d" % t, [P, S], F32) for t in range(PACK)]
+        st_n4 = [reused("st_n4%d" % t, "n4%d" % t, [P, S], F32) for t in range(PACK)]
+        low = [reused("low%d" % t, "low%d" % t, [P, S], F32) for t in range(PACK)]
+        z2_p = sb("z2_p", [P, PACK, S], BF16)
+        pa, old = {}, {}
 
-        def pick(t):
-            s_copy(picked[t // 2][:, 0, t % 2, :], y_sb[t][:].indirect(l_n2[:]))
-            s_copy(picked[t // 2][:, 1, t % 2, :], y_sb[t][:].indirect(l_n1[:]))
-
-        pick(0)
-        for t in range(PACK):
-            s_copy(d_n3[t // 2][:, t % 2, :], d_sb[t][:].indirect(l_n3[:]))
-        pick(1)
-        picked.append(reused("picked1", "d3", [P, 2, 2, W], F32))
-        pick(2)
-        pick(3)
-        w3d = deal("w3d", w3w, U32, 4)
-        w4d = deal("w4d", w4w, U32, 4)
-        ra = [reused("ra0", "d1", [P, 2, W], F32)]
-
-        def larger(u):
-            nc.vector.scalar_tensor_tensor(
-                out=flat(ra[u]), in0=flat(picked[u][:, 1]), scalar=0.5, in1=flat(picked[u][:, 0]),
-                op0=ALU.mult, op1=ALU.max)
-
-        def upper(u):
-            for a in range(2):
-                nc.vector.tensor_tensor(st_sb[u][:, a * S : (a + 1) * S], d_ps[2 * u + a][:], d_n3[u][:, a, :], ALU.max)
+        def upper(t):
+            nc.vector.tensor_tensor(st_sb[t % 2][:, :S], d_ps[t][:], d_n3[t][:], ALU.max)
 
         def fetch(t):
-            a = t % 2
-            nc.vector.tensor_copy(st_n4[t // 2][:, a, :], st_sb[t // 2][:, a * S : (a + 2) * S].indirect(l_n4[:]))
+            nc.vector.tensor_copy(st_n4[t][:], st_sb[t % 2][:].indirect(l_n4[:]))
 
-        def lower(u):
-            nc.vector.tensor_tensor(flat(low[:, 2 * u : 2 * u + 2, :]), st_sb[u][:, : 2 * S], flat(st_n4[u]), ALU.min)
+        def lower(t):
+            nc.vector.tensor_tensor(low[t][:], st_sb[t % 2][:, :S], st_n4[t][:], ALU.min)
 
+        def gain2(t):
+            nc.vector.tensor_scalar(z2_p[:, t, :], low[t][:], g_m[:, t : t + 1], None, ALU.mult)
+
+        def larger(planes, tag):
+            u, a, n = planes[0] // 2, planes[0] % 2, len(planes)
+            tile = reused("ra%d" % planes[0], tag, [P, n, W], F32)
+            nc.vector.scalar_tensor_tensor(
+                out=tile[:], in0=old[u][:, a : a + n, :], scalar=0.5, in1=pa[u][:, a : a + n, :],
+                op0=ALU.mult, op1=ALU.max)
+            for i, t in enumerate(planes):
+                s_copy(y_sb[t][:].indirect(l_n1[:]), tile[:, i, :])
+
+        def weave(dst, src):
+            nc.vector.tensor_copy(
+                dst.rearrange("p (c i) t -> p c t i", i=4), src.rearrange("p t (c i) -> p c t i", i=4))
+
+        def quantise(words, scales, src):
+            nc.vector.quantize_mx(out=words.bitcast(FP8X4), scales=scales, in_=src.rearrange("p j t -> p (j t)"))
+
+        picked0 = sb("picked0", [P, 2, 2, W], F32)
+        pa[0], old[0] = picked0[:, 0], picked0[:, 1]
+        for t in range(2):
+            s_copy(pa[0][:, t, :], y_sb[t][:].indirect(l_n2[:]))
+            s_copy(old[0][:, t, :], y_sb[t][:].indirect(l_n1[:]))
+        for t in range(PACK):
+            s_copy(d_n3[t][:], d_sb[t][:].indirect(l_n3[:]))
+        picked1 = reused("picked1", "d2", [P, 2, 2, W], F32)
+        pa[1], old[1] = picked1[:, 0], picked1[:, 1]
+        for t in range(2):
+            s_copy(pa[1][:, t, :], y_sb[2 + t][:].indirect(l_n2[:]))
+            s_copy(old[1][:, t, :], y_sb[2 + t][:].indirect(l_n1[:]))
+
+        w4d = deal("w4d", w4w, U32, 4)
         upper(0)
-        larger(0)
+        w3d = deal("w3d", w3w, U32, 4)
+        upper(1)
+        larger((0, 1), "d0")
         fetch(0)
         fetch(1)
-        upper(1)
         lower(0)
-        fetch(2)
-        ra.append(reused("ra1", "n40", [P, 2, W], F32))
-        larger(1)
-        fetch(3)
-        for t in range(PACK):
-            s_copy(y_sb[t][:].indirect(l_n1[:]), ra[t // 2][:, t % 2, :])
         lower(1)
+        upper(2)
+        upper(3)
+        gain2(0)
+        gain2(1)
+        fetch(2)
+        larger((2,), "d_n32")
+        fetch(3)
+        lower(2)
+        lower(3)
+        gain2(2)
+        gain2(3)
+        larger((3,), "low2")
 
-        z2_b = sb("z2_b", [P, S * PACK], BF16)
-        nc.vector.tensor_tensor(
-            z2_b[:].rearrange("p (c i t) -> p c t i", t=PACK, i=4),
-            low[:].rearrange("p t (c i) -> p c t i", i=4),
-            g_m[:].unsqueeze(1).unsqueeze(3).broadcast_to([P, S // 4, PACK, 4]),
-            ALU.mult)
-        z_b = reused("z_b", "n41", [P, S, PACK], BF16)
+        z2_b = sb("z2_b", [P, S, PACK], BF16)
         z2w = sb("z2w", [P, S], U32)
         z2s = sb("z2s", [P, S], U8)
         zw = sb("zw", [P, S], U32)
         zs = sb("zs", [P, S], U8)
+        weave(z2_b[:], z2_p[:])
+        quantise(z2w[:], z2s[:], z2_b[:])
+        z_b = reused("z_b", "n43", [P, S, PACK], BF16)
         for t in range(PACK - 1):
             nc.vector.tensor_scalar(z_b[:, :, t], y_sb[t][:], g_n[:, t : t + 1], None, ALU.mult)
-            if t == 0:
-                nc.vector.quantize_mx(out=z2w[:].bitcast(FP8X4), scales=z2s[:], in_=z2_b[:])
         h_ps = [psum.tile([P, S], F32, name="h_ps%d" % t, tag="bank%d" % t) for t in range(PACK)]
         for t in range(PACK):
             product(h_ps[t][:], w4d, s234d, 8, t, z2w, z2s, True, False)
         t = PACK - 1
         nc.vector.tensor_scalar(z_b[:, :, t], y_sb[t][:], g_n[:, t : t + 1], None, ALU.mult)
-        nc.vector.quantize_mx(out=zw[:].bitcast(FP8X4), scales=zs[:], in_=z_b[:].rearrange("p j t -> p (j t)"))
+        quantise(zw[:], zs[:], z_b[:])
         for t in range(PACK):
             product(h_ps[t][:], w3d, s234d, 4, t, zw, zs, False, True)
 

@@ -30,7 +30,6 @@ def tile_picked_hjoinkmaxhopmndif_none_po_kernel(
     nc = tc.nc
     with ExitStack() as ctx:
         keep = ctx.enter_context(tc.tile_pool(name="keep", bufs=1))
-        shared = ctx.enter_context(tc.tile_pool(name="shared", bufs=1))
         psum = ctx.enter_context(tc.psum_pool(name="psum", bufs=1))
 
         def sb(name, shape, dtype):
@@ -61,7 +60,7 @@ def tile_picked_hjoinkmaxhopmndif_none_po_kernel(
             cols = slice(P * t, P * (t + 1))
             nc.tensor.matmul_mx(
                 out=acc, lhsT=words[:, cols].bitcast(FP8X4), lhsT_scale=scales[row0:P, cols],
-                rhs=rhs[:].bitcast(FP8X4), rhs_scale=rhs_scale[:], start=start, stop=stop,
+                rhs=rhs[:].bitcast(FP8X4), rhs_scale=rhs_scale, start=start, stop=stop,
             )
 
         def reused(name, tag, shape, dtype):
@@ -76,80 +75,63 @@ def tile_picked_hjoinkmaxhopmndif_none_po_kernel(
         def flat(tile):
             return tile[:].rearrange("p a j -> p (a j)")
 
-        xs = sb("xs", [P, T], U8)
+        xs = reused("xs", "xs", [P, T], U8)
         nc.vector.memset(xs[:].bitcast(I32), 0)
-        stage1 = sb("stage1", [32, H], I32)
-        nc.vector.memset(stage1[:], 0)
-        stage234 = reused("stage234", "stage234", [32, H], I32)
-        nc.vector.memset(stage234[:], 0)
-        d_sb = [reused("d_sb%d" % t, "d%d" % t, [P, S + SPARE], F32) for t in range(PACK)]
+        stage = sb("stage", [32, H], I32)
+        nc.vector.memset(stage[:], 0)
+        xs_placed = sb("xs_placed", [P, 2 * S], U8)
+        nc.vector.memset(xs_placed[:].bitcast(I32), 0)
+        d_sb = [sb("d_sb%d" % t, [P, S + SPARE], F32) for t in range(PACK)]
         st_sb = [sb("st_sb%d" % u, [P, S + WIDE_SPARE], F32) for u in range(2)]
-        for tile in d_sb:
-            nc.vector.memset(tile[:, S:], 0.0)
-        for tile in st_sb:
+        for tile in d_sb + st_sb:
             nc.vector.memset(tile[:, S:], 0.0)
 
+        w2w = load_words(nc.gpsimd, "w2w", w2_words)
         l_offs = load_list("l_offs", offs)
         l_hz = load_list("l_hz", hz)
-        xs_rows = x_scales[0].bitcast(I32)
-        xs_i = xs[:].bitcast(I32)
-        for r in range(2):
-            nc.scalar.dma_start(xs_i[r:P:32, :], xs_rows[r:16:4, :])
-        for r, queue in ((2, nc.scalar), (3, nc.sync)):
-            queue.dma_start(xs_i[r:P:16, :], xs_rows[r:16:4, :].unsqueeze(1).broadcast_to([4, 2, T // 4]))
-        stage_scales(nc.sync, stage1, 0, w1_scales)
+        nc.sync.dma_start(xs[:].bitcast(I32)[0:P:8, :], x_scales[0].bitcast(I32))
+        for w, src in enumerate((w1_scales, w2_scales, w3_scales, w4_scales)):
+            stage_scales(nc.sync if w < 2 else nc.scalar, stage, w, src)
         xw = load_words(nc.sync, "xw", x_words)
-        for w, src in enumerate((w2_scales, w3_scales, w4_scales)):
-            stage_scales(nc.sync, stage234, w, src)
+        ws = reused("ws", "ws", [P, H], U8)
+        spread_scales(nc.sync, ws, stage)
         w1w = load_words(nc.sync, "w1w", w1_words)
-        l_n2 = load_list("l_n2", n2)
-        w2w = load_words(nc.sync, "w2w", w2_words)
-        l_n1 = load_list("l_n1", n1)
-        s1 = reused("s1", "s1", [P, H], U8)
-        spread_scales(nc.scalar, s1, stage1)
-        s234 = shared.tile([P, H], U8, name="s234", offset=4 * S - H // 2, align_bytes=64)
-        spread_scales(nc.sync, s234, stage234)
-        g_n = sb("g_n", [P, PACK], F32)
-        g_m = sb("g_m", [P, PACK], F32)
-        nc.gpsimd.dma_start(g_m[:], gm.rearrange("(p t) o -> p (t o)", t=PACK))
-        nc.gpsimd.dma_start(g_n[:], gn.rearrange("(p t) o -> p (t o)", t=PACK))
-
-        xs_offs = sb("xs_offs", [P, S], U8)
-        nc.vector.tensor_copy(xs_offs[:], xs[:].indirect(l_offs[:]))
-        xs_hz = sb("xs_hz", [P, S], U8)
-        nc.vector.tensor_copy(xs_hz[:], xs[:].indirect(l_hz[:]))
-        xs_hz_placed = sb("xs_hz_placed", [P, S], U8)
-        nc.vector.tensor_copy(xs_hz_placed[:].bitcast(I32), xs_hz[:].bitcast(I32))
-        for r in range(2, 4):
-            nc.sync.dma_start(xs_hz_placed[:].bitcast(I32)[r:P:32, :], xs_hz[:].bitcast(I32)[16 + r : P : 32, :])
         l_n3 = load_list("l_n3", n3)
+        l_n2 = load_list("l_n2", n2)
+        l_n1 = load_list("l_n1", n1)
+        l_n4 = load_list("l_n4", n4)
         w4w = load_words(nc.sync, "w4w", w4_words)
         w3w = load_words(nc.sync, "w3w", w3_words)
-        l_n4 = load_list("l_n4", n4)
+        g_n = sb("g_n", [P, PACK], F32)
+        g_m = sb("g_m", [P, PACK], F32)
+        nc.sync.dma_start(g_m[:], gm.rearrange("(p t) o -> p (t o)", t=PACK))
+        nc.sync.dma_start(g_n[:], gn.rearrange("(p t) o -> p (t o)", t=PACK))
         l_n5 = load_list("l_n5", n5)
 
-        xw_offs = sb("xw_offs", [P, S], U32)
-        nc.vector.tensor_copy(xw_offs[:], xw[:].indirect(l_offs[:]))
-        s1d = deal("s1d", s1, U8, 16)
-        w1d = deal("w1d", w1w, U32, 4)
-        xw_hz = reused("xw_hz", "w1w", [P, S], U32)
+        xs_got = sb("xs_got", [P, 2 * S], U8)
+        nc.vector.tensor_copy(xs_got[:, :S], xs[:].indirect(l_hz[:]))
+        nc.vector.tensor_copy(xs_got[:, S:], xs[:].indirect(l_offs[:]))
+        for r in range(4):
+            nc.scalar.dma_start(xs_placed[:].bitcast(I32)[r:P:32, :], xs_got[:].bitcast(I32)[8 * r : P : 32, :])
+        w2d = deal("w2d", w2w, U32, 4, "xs")
+        xw_hz = sb("xw_hz", [P, S], U32)
         nc.vector.tensor_copy(xw_hz[:], xw[:].indirect(l_hz[:]))
-        w2d = deal("w2d", w2w, U32, 4, "xw")
-        s234d = deal("s234d", s234, U8, 16)
+        wsd = deal("wsd", ws, U8, 16)
+        xw_offs = reused("xw_offs", "ws", [P, S], U32)
+        nc.vector.tensor_copy(xw_offs[:], xw[:].indirect(l_offs[:]))
+        w1d = deal("w1d", w1w, U32, 4)
 
         y_ps = [psum.tile([P, S], F32, name="y_ps%d" % t, tag="bank%d" % t) for t in range(PACK)]
         d_ps = [psum.tile([P, S], F32, name="d_ps%d" % t) for t in range(PACK)]
-        y_sb = [sb("y_sb0", [P, S], F32), reused("y_sb1", "stage234", [P, S], F32)]
-        y_sb += [shared.tile([P, S], F32, name="y_sb%d" % t, offset=4 * S * (t - 2), align_bytes=64) for t in (2, 3)]
         for t in range(PACK):
-            product(y_ps[t][:], w1d, s1d, 0, t, xw_offs, xs_offs, True, True)
-        for t in range(PACK):
-            product(d_ps[t][:], w2d, s234d, 0, t, xw_hz, xs_hz_placed, True, True)
-        nc.scalar.copy(y_sb[0][:], y_ps[0][:])
-        nc.vector.tensor_copy(y_sb[1][:], y_ps[1][:])
-        for t in range(PACK):
+            product(d_ps[t][:], w2d, wsd, 4, t, xw_hz, xs_placed[:, :S], True, True)
+        nc.scalar.copy(d_sb[0][:, :S], d_ps[0][:])
+        for t in range(1, PACK):
             nc.vector.tensor_copy(d_sb[t][:, :S], d_ps[t][:])
-        for t in range(2, PACK):
+        y_sb = [sb("y_sb%d" % t, [P, S], F32) for t in range(PACK)]
+        for t in range(PACK):
+            product(y_ps[t][:], w1d, wsd, 0, t, xw_offs, xs_placed[:, S:], True, True)
+        for t in range(PACK):
             nc.vector.tensor_copy(y_sb[t][:], y_ps[t][:])
 
         d_n3 = [reused("d_n3%d" % t, "d_n3%d" % t, [P, S], F32) for t in range(PACK)]
@@ -186,59 +168,56 @@ def tile_picked_hjoinkmaxhopmndif_none_po_kernel(
         def quantise(words, scales, src):
             nc.vector.quantize_mx(out=words.bitcast(FP8X4), scales=scales, in_=src.rearrange("p j t -> p (j t)"))
 
-        picked0 = sb("picked0", [P, 2, 2, W], F32)
-        pa[0], old[0] = picked0[:, 0], picked0[:, 1]
-        for t in range(2):
-            s_copy(pa[0][:, t, :], y_sb[t][:].indirect(l_n2[:]))
-            s_copy(old[0][:, t, :], y_sb[t][:].indirect(l_n1[:]))
         for t in range(PACK):
             s_copy(d_n3[t][:], d_sb[t][:].indirect(l_n3[:]))
-        picked1 = reused("picked1", "d2", [P, 2, 2, W], F32)
-        pa[1], old[1] = picked1[:, 0], picked1[:, 1]
-        for t in range(2):
-            s_copy(pa[1][:, t, :], y_sb[2 + t][:].indirect(l_n2[:]))
-            s_copy(old[1][:, t, :], y_sb[2 + t][:].indirect(l_n1[:]))
+        for u in range(2):
+            picked = sb("picked%d" % u, [P, 2, 2, W], F32)
+            pa[u], old[u] = picked[:, 0], picked[:, 1]
+            for a in range(2):
+                s_copy(pa[u][:, a, :], y_sb[2 * u + a][:].indirect(l_n2[:]))
+                s_copy(old[u][:, a, :], y_sb[2 * u + a][:].indirect(l_n1[:]))
 
-        w4d = deal("w4d", w4w, U32, 4)
         upper(0)
-        w3d = deal("w3d", w3w, U32, 4)
         upper(1)
-        larger((0, 1), "d0")
         fetch(0)
         fetch(1)
         lower(0)
         lower(1)
+        larger((0, 1), "n40")
         upper(2)
         upper(3)
         gain2(0)
         gain2(1)
         fetch(2)
-        larger((2,), "d_n32")
+        larger((2, 3), "d_n33")
         fetch(3)
         lower(2)
         lower(3)
         gain2(2)
         gain2(3)
-        larger((3,), "low2")
+        w4d = deal("w4d", w4w, U32, 4, "n41")
+        w3d = deal("w3d", w3w, U32, 4, "n42")
 
-        z2_b = sb("z2_b", [P, S, PACK], BF16)
+        z2_b = reused("z2_b", "woven", [P, S, PACK], BF16)
         z2w = sb("z2w", [P, S], U32)
         z2s = sb("z2s", [P, S], U8)
         zw = sb("zw", [P, S], U32)
         zs = sb("zs", [P, S], U8)
         weave(z2_b[:], z2_p[:])
         quantise(z2w[:], z2s[:], z2_b[:])
-        z_b = reused("z_b", "n43", [P, S, PACK], BF16)
-        for t in range(PACK - 1):
-            nc.vector.tensor_scalar(z_b[:, :, t], y_sb[t][:], g_n[:, t : t + 1], None, ALU.mult)
+        z_p = reused("z_p", "n43", [P, 2, S], BF16)
+        z_b = reused("z_b", "woven", [P, S, PACK], BF16)
+        for t in range(2):
+            nc.vector.tensor_scalar(z_p[:, t, :], y_sb[t][:], g_n[:, t : t + 1], None, ALU.mult)
+        weave(z_b[:, :, :2], z_p[:])
         h_ps = [psum.tile([P, S], F32, name="h_ps%d" % t, tag="bank%d" % t) for t in range(PACK)]
         for t in range(PACK):
-            product(h_ps[t][:], w4d, s234d, 8, t, z2w, z2s, True, False)
-        t = PACK - 1
-        nc.vector.tensor_scalar(z_b[:, :, t], y_sb[t][:], g_n[:, t : t + 1], None, ALU.mult)
+            product(h_ps[t][:], w4d, wsd, 12, t, z2w, z2s[:], True, False)
+        for t in range(2, PACK):
+            nc.vector.tensor_scalar(z_b[:, :, t], y_sb[t][:], g_n[:, t : t + 1], None, ALU.mult)
         quantise(zw[:], zs[:], z_b[:])
         for t in range(PACK):
-            product(h_ps[t][:], w3d, s234d, 4, t, zw, zs, False, True)
+            product(h_ps[t][:], w3d, wsd, 8, t, zw, zs[:], False, True)
 
         h_sb = sb("h_sb", [P, PACK, S], F32)
         for t in range(PACK):
@@ -255,7 +234,7 @@ def tile_picked_hjoinkmaxhopmndif_none_po_kernel(
             for t in range(PACK):
                 window = flat(h_sb)[:, t * S : (PACK if half else t + 1) * S]
                 s_copy(h_n5[:, t, :], window.indirect(l_n5[:, half * 8 : (half + 1) * 8]))
-            for pair in (slice(0, 3), slice(3, 4)) if half else (slice(0, PACK),):
+            for pair in (slice(0, 2), slice(2, 3), slice(3, 4)) if half else (slice(0, 2), slice(2, 4)):
                 nc.vector.tensor_tensor(res[:, pair, cols], h_sb[:, pair, cols], h_n5[:, pair, :], ALU.subtract)
             nc.scalar.dma_start(out_rows[:, :, cols], res[:, :, cols])
             wide = slice(half * HALF * PACK, (half + 1) * HALF * PACK)

from contextlib import ExitStack

import concourse.mybir as mybir

K, T, S, H, N, W = 512, 2048, 256, 512, 512, 192
FLOPS = 4 * 2 * K * H * S

F32 = mybir.dt.float32
BF16 = mybir.dt.bfloat16
I32 = mybir.dt.int32
U32 = mybir.dt.uint32
U16 = mybir.dt.uint16
U8 = mybir.dt.uint8
FP8X4 = mybir.dt.float8_e4m3fn_x4
ALU = mybir.AluOpType
COPY = mybir.ActivationFunctionType.Copy

P = 128
PACK = 4
HALF = S // 2
SPARE = 16
WIDE_SPARE = 96


def tile_picked_hjoinkmaxhopmndif_none_po_kernel(
    tc, x_words, x_scales, w1_words, w1_scales, w2_words, w2_scales, gn, gm,
    w3_words, w3_scales, w4_words, w4_scales, offs, hz, n1, n2, n3, n4, n5,
    out_0, out_1, out_2,
):
    nc = tc.nc
    with ExitStack() as ctx:
        keep = ctx.enter_context(tc.tile_pool(name="keep", bufs=1))
        psum = ctx.enter_context(tc.psum_pool(name="psum", bufs=1))

        def sb(name, shape, dtype):
            return keep.tile(shape, dtype, name=name, align_bytes=64)

        def load_list(name, src):
            tile = keep.tile(list(src.shape), U16, name=name)
            nc.sync.dma_start(tile[:], src)
            return tile

        def load_words(queue, name, src, tag=None):
            tile = keep.tile([P, src.shape[2]], U32, name=name, tag=tag or name, align_bytes=64)
            queue.dma_start(tile[:].bitcast(I32), src[0].rearrange("p c r -> p (c r)").bitcast(I32))
            return tile

        def deal(name, src, dtype, run, tag=None):
            tile = keep.tile([P, H], dtype, name=name, tag=tag or name, align_bytes=64)
            nc.vector.tensor_copy(
                out=tile[:].rearrange("p (t c i) -> p c t i", t=PACK, i=run),
                in_=src[:].rearrange("p (c i t) -> p c t i", t=PACK, i=run),
            )
            return tile

        def s_copy(out, in_):
            nc.scalar.activation(out, in_, COPY)

        def product(acc, words, scales, row0, t, rhs, rhs_scale, start, stop):
            cols = slice(P * t, P * (t + 1))
            nc.tensor.matmul_mx(
                out=acc, lhsT=words[:, cols].bitcast(FP8X4), lhsT_scale=scales[row0:P, cols],
                rhs=rhs[:].bitcast(FP8X4), rhs_scale=rhs_scale, start=start, stop=stop,
            )

        def reused(name, tag, shape, dtype):
            return keep.tile(shape, dtype, name=name, tag=tag, align_bytes=64)

        def stage_scales(queue, stage, w, src):
            queue.dma_start(stage[w:32:8, :], src[0].rearrange("(q r) c -> q (r c)", r=4).bitcast(I32))

        def spread_scales(queue, tile, stage):
            queue.dma_start(tile[:].bitcast(I32), stage[:].rearrange("g (r c) -> g r c", r=4))

        def flat(tile):
            return tile[:].rearrange("p a j -> p (a j)")

        xs = reused("xs", "xs", [P, T], U8)
        nc.vector.memset(xs[:].bitcast(I32), 0)
        stage = sb("stage", [32, H], I32)
        nc.vector.memset(stage[:], 0)
        xs_placed = sb("xs_placed", [P, 2 * S], U8)
        nc.vector.memset(xs_placed[:].bitcast(I32), 0)
        d_sb = [sb("d_sb%d" % t, [P, S + SPARE], F32) for t in range(PACK)]
        st_sb = [sb("st_sb%d" % u, [P, S + WIDE_SPARE], F32) for u in range(2)]
        for tile in d_sb + st_sb:
            nc.vector.memset(tile[:, S:], 0.0)

        w2w = load_words(nc.gpsimd, "w2w", w2_words)
        l_offs = load_list("l_offs", offs)
        l_hz = load_list("l_hz", hz)
        nc.sync.dma_start(xs[:].bitcast(I32)[0:P:8, :], x_scales[0].bitcast(I32))
        for w, src in enumerate((w1_scales, w2_scales, w3_scales, w4_scales)):
            stage_scales(nc.sync if w < 2 else nc.scalar, stage, w, src)
        xw = load_words(nc.sync, "xw", x_words)
        ws = reused("ws", "ws", [P, H], U8)
        spread_scales(nc.sync, ws, stage)
        w1w = load_words(nc.sync, "w1w", w1_words)
        l_n3 = load_list("l_n3", n3)
        l_n2 = load_list("l_n2", n2)
        l_n1 = load_list("l_n1", n1)
        l_n4 = load_list("l_n4", n4)
        w4w = load_words(nc.sync, "w4w", w4_words)
        w3w = load_words(nc.sync, "w3w", w3_words)
        g_n = sb("g_n", [P, PACK], F32)
        g_m = sb("g_m", [P, PACK], F32)
        nc.sync.dma_start(g_m[:], gm.rearrange("(p t) o -> p (t o)", t=PACK))
        nc.sync.dma_start(g_n[:], gn.rearrange("(p t) o -> p (t o)", t=PACK))
        l_n5 = load_list("l_n5", n5)

        xs_got = sb("xs_got", [P, 2 * S], U8)
        nc.vector.tensor_copy(xs_got[:, :S], xs[:].indirect(l_hz[:]))
        nc.vector.tensor_copy(xs_got[:, S:], xs[:].indirect(l_offs[:]))
        for r in range(4):
            nc.scalar.dma_start(xs_placed[:].bitcast(I32)[r:P:32, :], xs_got[:].bitcast(I32)[8 * r : P : 32, :])
        w2d = deal("w2d", w2w, U32, 4, "xs")
        xw_hz = sb("xw_hz", [P, S], U32)
        nc.vector.tensor_copy(xw_hz[:], xw[:].indirect(l_hz[:]))
        wsd = deal("wsd", ws, U8, 16)
        xw_offs = reused("xw_offs", "ws", [P, S], U32)
        nc.vector.tensor_copy(xw_offs[:], xw[:].indirect(l_offs[:]))
        w1d = deal("w1d", w1w, U32, 4)

        y_ps = [psum.tile([P, S], F32, name="y_ps%d" % t, tag="bank%d" % t) for t in range(PACK)]
        d_ps = [psum.tile([P, S], F32, name="d_ps%d" % t) for t in range(PACK)]
        for t in range(PACK):
            product(d_ps[t][:], w2d, wsd, 4, t, xw_hz, xs_placed[:, :S], True, True)
        nc.scalar.copy(d_sb[0][:, :S], d_ps[0][:])
        for t in range(1, PACK):
            nc.vector.tensor_copy(d_sb[t][:, :S], d_ps[t][:])
        y_sb = [sb("y_sb%d" % t, [P, S], F32) for t in range(PACK)]
        for t in range(PACK):
            product(y_ps[t][:], w1d, wsd, 0, t, xw_offs, xs_placed[:, S:], True, True)
        for t in range(PACK):
            nc.vector.tensor_copy(y_sb[t][:], y_ps[t][:])

        d_n3 = [reused("d_n3%d" % t, "d_n3%d" % t, [P, S], F32) for t in range(PACK)]
        st_n4 = [reused("st_n4%d" % t, "n4%d" % t, [P, S], F32) for t in range(PACK)]
        low = [reused("low%d" % t, "low%d" % t, [P, S], F32) for t in range(PACK)]
        z2_p = sb("z2_p", [P, PACK, S], BF16)
        pa, old = {}, {}

        def upper(t):
            nc.vector.tensor_tensor(st_sb[t % 2][:, :S], d_ps[t][:], d_n3[t][:], ALU.max)

        def fetch(t):
            nc.vector.tensor_copy(st_n4[t][:], st_sb[t % 2][:].indirect(l_n4[:]))

        def lower(t):
            nc.vector.tensor_tensor(low[t][:], st_sb[t % 2][:, :S], st_n4[t][:], ALU.min)

        def gain2(t):
            nc.vector.tensor_scalar(z2_p[:, t, :], low[t][:], g_m[:, t : t + 1], None, ALU.mult)

        def larger(planes, tag):
            u, a, n = planes[0] // 2, planes[0] % 2, len(planes)
            tile = reused("ra%d" % planes[0], tag, [P, n, W], F32)
            nc.vector.scalar_tensor_tensor(
                out=tile[:], in0=old[u][:, a : a + n, :], scalar=0.5, in1=pa[u][:, a : a + n, :],
                op0=ALU.mult, op1=ALU.max)
            for i, t in enumerate(planes):
                s_copy(y_sb[t][:].indirect(l_n1[:]), tile[:, i, :])

        def weave(dst, src):
            nc.vector.tensor_copy(
                dst.rearrange("p (c i) t -> p c t i", i=4), src.rearrange("p t (c i) -> p c t i", i=4))

        def quantise(words, scales, src):
            nc.vector.quantize_mx(out=words.bitcast(FP8X4), scales=scales, in_=src.rearrange("p j t -> p (j t)"))

        for t in range(PACK):
            s_copy(d_n3[t][:], d_sb[t][:].indirect(l_n3[:]))
        for u in range(2):
            picked = sb("picked%d" % u, [P, 2, 2, W], F32)
            pa[u], old[u] = picked[:, 0], picked[:, 1]
            for a in range(2):
                s_copy(pa[u][:, a, :], y_sb[2 * u + a][:].indirect(l_n2[:]))
                s_copy(old[u][:, a, :], y_sb[2 * u + a][:].indirect(l_n1[:]))

        upper(0)
        upper(1)
        fetch(0)
        fetch(1)
        lower(0)
        lower(1)
        larger((0, 1), "n40")
        upper(2)
        upper(3)
        gain2(0)
        gain2(1)
        fetch(2)
        larger((2, 3), "d_n33")
        fetch(3)
        lower(2)
        lower(3)
        gain2(2)
        gain2(3)
        w4d = deal("w4d", w4w, U32, 4, "n41")
        w3d = deal("w3d", w3w, U32, 4, "n42")

        z2_b = reused("z2_b", "woven", [P, S, PACK], BF16)
        z2w = sb("z2w", [P, S], U32)
        z2s = sb("z2s", [P, S], U8)
        zw = sb("zw", [P, S], U32)
        zs = sb("zs", [P, S], U8)
        weave(z2_b[:], z2_p[:])
        quantise(z2w[:], z2s[:], z2_b[:])
        z_p = reused("z_p", "n43", [P, 2, S], BF16)
        z_b = reused("z_b", "woven", [P, S, PACK], BF16)
        for t in range(2):
            nc.vector.tensor_scalar(z_p[:, t, :], y_sb[t][:], g_n[:, t : t + 1], None, ALU.mult)
        weave(z_b[:, :, :2], z_p[:])
        h_ps = [psum.tile([P, S], F32, name="h_ps%d" % t, tag="bank%d" % t) for t in range(PACK)]
        for t in range(PACK):
            product(h_ps[t][:], w4d, wsd, 12, t, z2w, z2s[:], True, False)
        for t in range(2, PACK):
            nc.vector.tensor_scalar(z_b[:, :, t], y_sb[t][:], g_n[:, t : t + 1], None, ALU.mult)
        quantise(zw[:], zs[:], z_b[:])
        for t in range(PACK):
            product(h_ps[t][:], w3d, wsd, 8, t, zw, zs[:], False, True)

        h_sb = sb("h_sb", [P, PACK, S], F32)
        for t in range(PACK):
            nc.vector.tensor_copy(h_sb[:, t, :], h_ps[t][:])
        res = sb("res", [P, PACK, S], F32)
        res_b = sb("res_b", [P, S * PACK], BF16)
        res_w = sb("res_w", [P, S], U32)
        res_s = sb("res_s", [P, S], U8)
        out_rows = out_0.rearrange("(p t) j -> p t j", t=PACK)
        out_words = out_1[0].rearrange("p c r -> p (c r)").bitcast(I32)
        for half in range(2):
            cols = slice(half * HALF, (half + 1) * HALF)
            h_n5 = sb("h_n5%d" % half, [P, PACK, HALF], F32)
            for t in range(PACK):
                window = flat(h_sb)[:, t * S : (PACK if half else t + 1) * S]
                s_copy(h_n5[:, t, :], window.indirect(l_n5[:, half * 8 : (half + 1) * 8]))
            for pair in (slice(0, 2), slice(2, 3), slice(3, 4)) if half else (slice(0, 2), slice(2, 4)):
                nc.vector.tensor_tensor(res[:, pair, cols], h_sb[:, pair, cols], h_n5[:, pair, :], ALU.subtract)
            nc.scalar.dma_start(out_rows[:, :, cols], res[:, :, cols])
            wide = slice(half * HALF * PACK, (half + 1) * HALF * PACK)
            nc.vector.tensor_copy(
                res_b[:, wide].rearrange("p (c i t) -> p c t i", t=PACK, i=4),
                res[:, :, cols].rearrange("p t (c i) -> p c t i", i=4))
            nc.vector.quantize_mx(out=res_w[:, cols].bitcast(FP8X4), scales=res_s[:, cols], in_=res_b[:, wide])
            nc.sync.dma_start(out_words[:, cols], res_w[:, cols].bitcast(I32))
        out_scales = out_2[0].bitcast(I32)
        for r in range(4):
            queue = nc.scalar if r < 2 else nc.sync
            queue.dma_start(out_scales[r:16:4, :], res_s[:].bitcast(I32)[r:P:32, :])
